import numpy as np
import ml_dtypes


def mxq(x, axis, fmt="e4m3"):
    dtype, down = {"e4m3": (ml_dtypes.float8_e4m3fn, 7), "e5m2": (ml_dtypes.float8_e5m2, 14)}[fmt]
    v = np.moveaxis(np.asarray(x, np.float32).astype(ml_dtypes.bfloat16).astype(np.float64), axis, -1)
    blocks = v.reshape(v.shape[:-1] + (-1, 32))
    amax = np.abs(blocks).max(-1, keepdims=True)
    byte = np.maximum(np.where(amax > 0, np.frexp(amax)[1] - 1 + 127, 0) - down, 1)
    scale = np.exp2(byte - 127.0)
    codes = (blocks / scale).astype(np.float32).astype(dtype).astype(np.float64)
    return np.moveaxis((codes * scale).reshape(v.shape), -1, axis)


WIDE = False


def mx_kscale(k):
    if not WIDE:
        return np.ones(k)
    levels = np.array([10, -10, 5, -5, 0])
    if k % 512:
        return np.exp2(np.random.permutation(np.resize(levels, k // 32))).repeat(32)
    a = np.empty((k // 512, 16))
    for p in range(k // 512):
        a[p, :8] = np.random.permutation(np.resize(levels, 8))
        for g in range(8):
            far = levels[np.abs(levels - a[p, g]) >= 10]
            a[p, g + 8] = far[np.random.randint(len(far))]
    return np.exp2(a.ravel()).repeat(32)


def f64(x):
    return np.asarray(x).astype(np.float64)


def striped(idx):
    return np.tile(idx.reshape(-1, 16).T, (8, 1)).astype(np.uint16)


def unstriped(offs):
    return offs[:16].T.reshape(-1).astype(np.int64)


E2M1 = np.array([0.0, 0.5, 1.0, 1.5, 2.0, 3.0, 4.0, 6.0, -0.0, -0.5, -1.0, -1.5, -2.0, -3.0, -4.0, -6.0])


def pack_weight(w, fmt):
    k, n = w.shape
    w = f64(np.asarray(w, np.float32).astype(ml_dtypes.bfloat16)).reshape(k // 32, 32, n)
    amax = np.abs(w).max(1)
    if fmt == "e4m3":
        byte = np.frexp(amax)[1] - 1 + 127 - 7
    else:
        mant, ex = np.frexp(amax / 6.0)
        byte = np.where(mant > 0.5, ex, ex - 1) + 127
    byte = np.clip(np.where(amax > 0, byte, 1), 1, 254)
    scaled = (w * np.exp2(127.0 - byte)[:, None, :]).reshape(k, n).astype(np.float32)
    by_word = np.ascontiguousarray(scaled.reshape(k // 512, 128, 4, n).transpose(0, 1, 3, 2))
    if fmt == "e4m3":
        words = by_word.astype(ml_dtypes.float8_e4m3fn).view(np.uint8)
    else:
        c = by_word.astype(ml_dtypes.float4_e2m1fn).view(np.uint8) & 0xF
        words = (c[..., 0::2] | (c[..., 1::2] << 4)).reshape(k // 512, 128, 2 * n)
    return np.ascontiguousarray(words), np.ascontiguousarray(byte.astype(np.uint8).reshape(k // 512, 16, n))


def unpack_weight(words, scales, fmt):
    g, _, n = scales.shape
    words = np.ascontiguousarray(words).reshape(g, 128, n, -1)
    if fmt == "e4m3":
        vals = words.view(ml_dtypes.float8_e4m3fn).astype(np.float64)
    else:
        nib = np.empty((g, 128, n, 4), np.uint8)
        nib[..., 0::2] = words & 0xF
        nib[..., 1::2] = words >> 4
        vals = E2M1[nib]
    vals = vals * np.repeat(np.exp2(scales.astype(np.float64) - 127.0), 8, axis=1)[..., None]
    return vals.transpose(0, 1, 3, 2).reshape(g * 512, n)


def gelu(v):
    return 0.5 * v * (1.0 + np.tanh(np.sqrt(2.0 / np.pi) * (v + 0.044715 * v**3)))


def striped8(idx):
    return np.concatenate([v.reshape(-1, 16).T for v in idx]).astype(np.uint16)


def unstriped8(offs):
    return np.stack([offs[16 * g:16 * g + 16].T.reshape(-1) for g in range(8)]).astype(np.int64)


def put_heads(h, wgs, idx8, t2):
    r = np.arange(h.shape[0])
    page = np.zeros((h.shape[0], t2))
    page[r[:, None], idx8[r % 512 // 64]] = wgs[r // 4 % 128] * h
    return page


def bf(x):
    return np.asarray(x, np.float32).astype(ml_dtypes.bfloat16)


def planes(Y):
    n, m = Y.shape
    b = f64(bf(Y)).reshape(n // 32, 32, m)
    amax = np.abs(b).max(1)
    byte = np.clip(np.where(amax > 0, np.frexp(amax)[1] - 1 + 127 - 7, 1), 1, 254)
    codes = (b * np.exp2(127.0 - byte)[:, None, :]).reshape(n, m).astype(np.float32).astype(ml_dtypes.float8_e4m3fn).view(np.uint8)
    words = codes.reshape(n // 512, 128, 4, m).transpose(0, 1, 3, 2)
    return np.ascontiguousarray(words), np.ascontiguousarray(byte.astype(np.uint8).reshape(n // 512, 16, m))


K, T, S, H, T2, P, N = 1024, 2048, 512, 1024, 1024, 512, 1024

def setup_inputs():
    n = np.random.standard_normal
    s = mx_kscale(K)[:, None]
    u = mx_kscale(H)[:, None]
    tab_words, tab_scales = pack_weight(n((K, T)) * s, "e4m3")
    w4_words, w4_scales = pack_weight(0.55 * n((K, H)) / np.sqrt(K) / s, "e2m1")
    col = np.exp(0.8 * n(N))
    w2 = 0.6 * n((H, N)) / np.sqrt(H) * np.minimum(col, 1.0) / u
    return {
        "tab_words": tab_words, "tab_scales": tab_scales,
        "offs": striped(np.random.permutation(T)[:S]),
        "w4_words": w4_words, "w4_scales": w4_scales,
        "amp": (1.2 * np.exp(0.3 * n(H)) * u[:, 0]).astype(np.float32),
        "shift": (0.3 * n(H) * u[:, 0]).astype(np.float32),
        "wgs": np.repeat(np.random.uniform(0.5, 2.0, (8, S)), 16, axis=0).astype(np.float32),
        "offs2": striped8(np.stack([np.random.permutation(T2)[:S] for _ in range(8)])),
        "offs3": striped(np.random.permutation(T2)[:P]),
        "joint": (0.5 * n((H, P)) * u).astype(np.float32),
        "w2": w2.astype(np.float32),
        "sound": (0.2 * n((N, P)) * col[:, None]).astype(np.float32),
    }

def reference(tab_words, tab_scales, offs, w4_words, w4_scales, amp, shift, wgs, offs2, offs3, joint, w2, sound):
    v = unpack_weight(tab_words, tab_scales, "e4m3")[:, unstriped(offs)]
    w4 = unpack_weight(w4_words, w4_scales, "e2m1")
    phase = w4.T @ v
    h = np.sin(phase) * f64(amp)[:, None] + f64(shift)[:, None]
    page = put_heads(h, f64(wgs), unstriped8(offs2), T2)
    x = page[:, unstriped(offs3)]
    z = mxq(x + f64(joint), 0, "e4m3")
    q = mxq(f64(w2), 0, "e4m3").T @ z
    y = q * np.cos(q) + f64(sound)
    words, scales = planes(y)
    return y, words, scales

@@ -1,0 +1,305 @@
+import math
+from contextlib import ExitStack
+
+import concourse.mybir as mybir
+
+K, T, S, H, T2, M, N = 1024, 2048, 512, 1024, 1024, 512, 1024
+FLOPS = 2 * K * H * S + 2 * H * N * M
+
+F32 = mybir.dt.float32
+BF16 = mybir.dt.bfloat16
+I32 = mybir.dt.int32
+U32 = mybir.dt.uint32
+U16 = mybir.dt.uint16
+U8 = mybir.dt.uint8
+E4M3 = mybir.dt.float8_e4m3fn_x4
+E2M1 = mybir.dt.float4_e2m1fn_x4
+ALU = mybir.AluOpType
+ACT = mybir.ActivationFunctionType
+
+P = 128
+PACK = 4
+PASS = P * PACK
+QUADS = 4
+HALF = 256
+SLICES = H // P
+
+
+def tile_list_rail_break_slots_kernel(
+    tc, tab_words, tab_scales, offs, w4_words, w4_scales, amp, shift, wgs, offs2, offs3, joint, w2, sound,
+    out_0, out_1, out_2,
+):
+    nc = tc.nc
+    with ExitStack() as ctx:
+        lists = ctx.enter_context(tc.tile_pool(name="lists", bufs=1))
+        keep = ctx.enter_context(tc.tile_pool(name="keep", bufs=1))
+        ring = ctx.enter_context(tc.tile_pool(name="ring", bufs=2))
+        psum = ctx.enter_context(tc.psum_pool(name="psum", bufs=8))
+
+        idx = lists.tile([P, S // 16], U16, name="idx")
+        idx2 = lists.tile([P, S // 16], U16, name="idx2")
+        idx3 = lists.tile([P, M // 16], U16, name="idx3")
+
+        tab_sc = keep.tile([P, 2, T], U8, name="tab_sc", tag="tab_sc", align_bytes=64)
+        w4_sc_raw = keep.tile([P, 2, H], U8, name="w4_sc_raw", tag="w4_sc_raw", align_bytes=64)
+        nc.vector.memset(tab_sc[:].rearrange("p a t -> p (a t)").bitcast(I32), 0)
+        nc.gpsimd.memset(w4_sc_raw[:].rearrange("p a t -> p (a t)").bitcast(I32), 0)
+
+        amp_sb = keep.tile([P, 2, PACK], F32, name="amp_sb")
+        shift_sb = keep.tile([P, 2, PACK], F32, name="shift_sb")
+        nc.sync.dma_start(idx[:], offs)
+        nc.scalar.dma_start(amp_sb[:], amp.rearrange("(b p i) -> p b i", b=2, i=PACK))
+        nc.sync.dma_start(idx2[:], offs2)
+        nc.scalar.dma_start(shift_sb[:], shift.rearrange("(b p i) -> p b i", b=2, i=PACK))
+        nc.sync.dma_start(idx3[:], offs3)
+        tab_w = [keep.tile([P, T], U32, name="tab_w%d" % a, tag="tab_w%d" % a, align_bytes=64) for a in range(2)]
+        w4_raw = keep.tile([P, 2, 2 * H], U8, name="w4_raw", tag="w4_raw", align_bytes=64)
+        nc.sync.dma_start(w4_raw[:].bitcast(I32), w4_words.rearrange("a p c -> p a c").bitcast(I32))
+        nc.sync.dma_start(tab_w[0][:].bitcast(I32), tab_words[0].rearrange("p t i -> p (t i)").bitcast(I32))
+        nc.sync.dma_start(tab_w[1][:].bitcast(I32), tab_words[1].rearrange("p t i -> p (t i)").bitcast(I32))
+        for q in range(QUADS):
+            nc.scalar.dma_start(
+                tab_sc[32 * q : 32 * q + 4, :, :].bitcast(I32),
+                tab_scales[:, 4 * q : 4 * q + 4, :].rearrange("a r t -> r a t").bitcast(I32),
+            )
+        for q in range(QUADS):
+            queue = nc.scalar if q < 2 else nc.gpsimd
+            queue.dma_start(
+                w4_sc_raw[32 * q : 32 * q + 4, :, :].bitcast(I32),
+                w4_scales[:, 4 * q : 4 * q + 4, :].rearrange("a r c -> r a c").bitcast(I32),
+            )
+        slope = keep.tile([P, 2, PACK], F32, name="slope")
+        level = keep.tile([P, 2, PACK], F32, name="level")
+        nc.gpsimd.tensor_scalar(slope[:], amp_sb[:], -2.0, 0.0, ALU.mult, ALU.add)
+        nc.gpsimd.tensor_tensor(level[:], amp_sb[:], shift_sb[:], ALU.add)
+
+        pages = {}
+
+        def new_page(s, engine):
+            pages[s] = keep.tile([P, T2], F32, name="page%d" % s, tag="page%d" % s)
+            engine.memset(pages[s][:], 0.0)
+
+        new_page(0, nc.vector)
+        new_page(1, nc.vector)
+
+        v_sc = keep.tile([P, 2, S], U8, name="v_sc", align_bytes=64)
+        v_w = [keep.tile([P, S], U32, name="v_w%d" % a, tag="v_w%d" % a, align_bytes=64) for a in range(2)]
+
+        w4_w = [keep.tile([P, 2, 2 * PASS], U8, name="w4_w%d" % b, tag="w4_w%d" % b, align_bytes=64) for b in range(2)]
+        w4_sc = [keep.tile([P, 2, PASS], U8, name="w4_sc%d" % b, tag="w4_sc%d" % b, align_bytes=64) for b in range(2)]
+
+        def deal_w4(b):
+            src = w4_raw[:].bitcast(U16)[:, :, b * PASS : (b + 1) * PASS]
+            nc.vector.tensor_copy(
+                w4_w[b][:].bitcast(U16).rearrange("p a (i u c) -> p a u i c", i=PACK, c=8),
+                src.rearrange("p a (u c i) -> p a u i c", i=PACK, c=8),
+            )
+            nc.vector.tensor_copy(
+                w4_sc[b][:].rearrange("p a (i u c) -> p a u i c", i=PACK, c=16),
+                w4_sc_raw[:, :, b * PASS : (b + 1) * PASS].rearrange("p a (u c i) -> p a u i c", i=PACK, c=16),
+            )
+
+        def gather_words(a, j0):
+            nc.vector.tensor_copy(
+                v_w[a][:, j0 : j0 + HALF], tab_w[a][:].indirect(idx[:, j0 // 16 : (j0 + HALF) // 16])
+            )
+
+        def gather_scales(a, j0):
+            nc.vector.tensor_copy(
+                v_sc[:, a, j0 : j0 + HALF], tab_sc[:, a, :].indirect(idx[:, j0 // 16 : (j0 + HALF) // 16])
+            )
+
+        deal_w4(0)
+        for j0 in (0, HALF):
+            for a in range(2):
+                gather_scales(a, j0)
+            for a in range(2):
+                gather_words(a, j0)
+        deal_w4(1)
+
+        def load_rows(name, tag, rows):
+            tile = keep.tile([P, PACK, PASS], F32, name=name, tag=tag, align_bytes=64)
+            nc.sync.dma_start(tile[:], rows.rearrange("(p i) m -> p i m", i=PACK))
+            return tile
+
+        def block(x, b, g):
+            return x[b * PASS : (b + 1) * PASS, g * PASS : (g + 1) * PASS]
+
+        wgs_sb = keep.tile([P, S], F32, name="wgs_sb", tag="tab_sc", align_bytes=64)
+        nc.sync.dma_start(wgs_sb[:], wgs)
+        joint_sb, w2_raw, sound_sb = {}, {}, {}
+        w2_tags = {(0, 0): "tab_w1", (1, 0): "w4_raw", (0, 1): "w4_sc_raw", (1, 1): "w4_w0"}
+        joint_sb[0] = load_rows("joint0", "tab_w0", block(joint, 0, 0))
+        for b, g in ((0, 0), (1, 0), (0, 1)):
+            w2_raw[b, g] = load_rows("w2_raw%d%d" % (b, g), w2_tags[b, g], block(w2, b, g))
+
+        z_first = [keep.tile([P, PACK, S], F32, name="z_first%d" % b) for b in range(2)]
+        h = {}
+
+        def region(s):
+            return z_first[s // PACK][:, s % PACK, :]
+
+        def make_h(s, j0, j1):
+            b, i = divmod(s, PACK)
+            phase = psum.tile([P, j1 - j0], F32, name="phase", tag="bank")
+            for a in range(2):
+                nc.tensor.matmul_mx(
+                    out=phase[:],
+                    lhsT=w4_w[b][:, a, 2 * P * i : 2 * P * (i + 1)].bitcast(E2M1),
+                    lhsT_scale=w4_sc[b][:, a, P * i : P * (i + 1)],
+                    rhs=v_w[a][:, j0:j1].bitcast(E4M3),
+                    rhs_scale=v_sc[:, a, j0:j1],
+                    start=(a == 0),
+                    stop=(a == 1),
+                )
+            scratch = region((s - 1) % SLICES)[:, j0:j1]
+            nc.scalar.activation(scratch, phase[:], ACT.Sin, bias=-math.pi / 4, scale=0.5)
+            nc.scalar.activation(scratch, scratch, ACT.Square)
+            nc.scalar.activation(
+                h[s][:, j0:j1], scratch, ACT.Identity, bias=level[:, b, i : i + 1], scale=slope[:, b, i : i + 1]
+            )
+
+        def scatter(s, j0, j1):
+            nc.vector.tensor_tensor(
+                pages[s][:].indirect(idx2[:, j0 // 16 : j1 // 16]), h[s][:, j0:j1], wgs_sb[:, j0:j1], ALU.mult
+            )
+
+        def pick(s, c, dst):
+            b, i = divmod(s, PACK)
+            m0 = c * HALF
+            nc.vector.tensor_tensor(
+                dst,
+                pages[s][:].indirect(idx3[:, m0 // 16 : (m0 + HALF) // 16]),
+                joint_sb[b][:, i, m0 : m0 + HALF],
+                ALU.add,
+            )
+
+        def interleave(engine_copy, dst, src):
+            engine_copy(
+                dst[:].rearrange("p (c u) t -> p c t u", u=4), src.rearrange("p t (c u) -> p c t u", u=4)
+            )
+
+        w2_w = keep.tile([P, 2, N], U32, name="w2_w", align_bytes=64)
+        w2_sc = keep.tile([P, 2, N], U8, name="w2_sc", align_bytes=64)
+
+        def quantize_w2(b, g):
+            rounded = ring.tile([P, PASS * PACK], BF16, name="w2_rounded", align_bytes=64)
+            dst = rounded[:].rearrange("p (t m j) -> p m j t", t=PACK, j=PACK)
+            src = w2_raw[b, g][:].rearrange("p j (m t) -> p m j t", t=PACK)
+            for m0 in (0, P // 2):
+                nc.scalar.copy(dst[:, m0 : m0 + P // 2], src[:, m0 : m0 + P // 2])
+            cols = slice(g * PASS, (g + 1) * PASS)
+            nc.vector.quantize_mx(out=w2_w[:, b, cols].bitcast(E4M3), scales=w2_sc[:, b, cols], in_=rounded[:])
+
+        z_w, z_sc = {}, {}
+
+        def quantize_z(b, c, src):
+            rounded = ring.tile([P, HALF, PACK], BF16, name="z_rounded", align_bytes=64)
+            interleave(nc.scalar.copy, rounded, src)
+            z_w[b, c] = keep.tile([P, HALF], U32, name="z_w%d%d" % (b, c), align_bytes=64)
+            z_sc[b, c] = keep.tile([P, HALF], U8, name="z_sc%d%d" % (b, c), align_bytes=64)
+            nc.vector.quantize_mx(
+                out=z_w[b, c][:].bitcast(E4M3), scales=z_sc[b, c][:], in_=rounded[:].rearrange("p m t -> p (m t)")
+            )
+
+        w2_parts = [(0, 0), (1, 0), (0, 1), (1, 1)]
+        for s in range(SLICES):
+            if s + 2 < SLICES:
+                tag = "page%d" % (s + 2)
+            elif s + 1 < SLICES:
+                tag = "h_spare"
+            else:
+                tag = "z_second"
+            h[s] = keep.tile([P, S], F32, name="h%d" % s, tag=tag)
+            spans = [(0, HALF), (HALF, S)] if s == 0 else [(0, S)]
+            for j0, j1 in spans:
+                make_h(s, j0, j1)
+            if s == PACK - 1:
+                w2_raw[1, 1] = load_rows("w2_raw11", w2_tags[1, 1], block(w2, 1, 1))
+                joint_sb[1] = load_rows("joint1", "w4_sc0", block(joint, 1, 0))
+            if s == SLICES - 1:
+                for g in range(2):
+                    sound_sb[g] = load_rows("sound%d" % g, "v_w%d" % g, block(sound, g, 0))
+            for j0, j1 in spans:
+                scatter(s, j0, j1)
+            if s + 2 < SLICES:
+                new_page(s + 2, nc.gpsimd)
+            if s >= 1:
+                pick(s - 1, 0, region(s - 1)[:, 0:HALF])
+            if 2 <= s < 2 + len(w2_parts):
+                quantize_w2(*w2_parts[s - 2])
+            if s == SLICES - 2:
+                quantize_z(0, 0, z_first[0][:, :, 0:HALF])
+        pick(SLICES - 1, 0, region(SLICES - 1)[:, 0:HALF])
+        quantize_z(1, 0, z_first[1][:, :, 0:HALF])
+
+        z_second = keep.tile([P, SLICES, HALF], F32, name="z_second", tag="z_second")
+        for s in range(SLICES):
+            pick(s, 1, z_second[:, s, :])
+
+        y = {}
+        for c in range(2):
+            for g in range(2):
+                y[c, g] = keep.tile([P, PACK, HALF], F32, name="y%d%d" % (c, g), tag=w2_tags[g, c], align_bytes=64)
+        y_sc = [keep.tile([P, 2, HALF], U8, name="y_sc%d" % c, align_bytes=64) for c in range(2)]
+        banks = [(c, g, t0) for c in range(2) for g in range(2) for t0 in (0, 2)]
+        first_scratch = keep.tile([P, 2 * HALF], F32, name="first_scratch", tag="h_spare")
+        neg = {}
+
+        def y_pair(k):
+            c, g, t0 = banks[k]
+            return y[c, g][:, t0 : t0 + 2, :]
+
+        def product(k):
+            c, g, t0 = banks[k]
+            q = psum.tile([P, 2 * HALF], F32, name="q", tag="bank")
+            for t in range(2):
+                cols = slice(g * PASS + (t0 + t) * P, g * PASS + (t0 + t + 1) * P)
+                for b in range(2):
+                    nc.tensor.matmul_mx(
+                        out=q[:, t * HALF : (t + 1) * HALF],
+                        lhsT=w2_w[:, b, cols].bitcast(E4M3),
+                        lhsT_scale=w2_sc[:, b, cols],
+                        rhs=z_w[b, c][:].bitcast(E4M3),
+                        rhs_scale=z_sc[b, c][:],
+                        start=(b == 0),
+                        stop=(b == 1),
+                    )
+            scratch = first_scratch[:] if k == 0 else y_pair(k - 1).rearrange("p t m -> p (t m)")
+            neg[k] = ring.tile([P, 2 * HALF], F32, name="neg", bufs=4)
+            nc.scalar.activation(scratch, q[:], ACT.Sin, scale=0.5)
+            nc.scalar.activation(neg[k][:], scratch, ACT.Square, scale=math.sqrt(2.0))
+            nc.vector.scalar_tensor_tensor(neg[k][:], neg[k][:], 1.0, q[:], ALU.subtract, ALU.mult)
+
+        def finish(k):
+            c, g, t0 = banks[k]
+            cols = slice(c * HALF, (c + 1) * HALF)
+            nc.vector.tensor_tensor(
+                y_pair(k), sound_sb[g][:, t0 : t0 + 2, cols], neg[k][:].rearrange("p (t m) -> p t m", t=2), ALU.subtract
+            )
+            rows = out_0[g * PASS : (g + 1) * PASS, cols].rearrange("(p t) m -> p t m", t=PACK)
+            nc.sync.dma_start(rows[:, t0 : t0 + 2, :], y_pair(k))
+            if t0 == 0:
+                return
+            rounded = ring.tile([P, HALF, PACK], BF16, name="y_rounded", align_bytes=64)
+            interleave(nc.vector.tensor_copy if c == g else nc.scalar.copy, rounded, y[c, g][:])
+            y_w = ring.tile([P, HALF], U32, name="y_w", align_bytes=64)
+            nc.vector.quantize_mx(
+                out=y_w[:].bitcast(E4M3), scales=y_sc[c][:, g, :], in_=rounded[:].rearrange("p m t -> p (m t)")
+            )
+            nc.sync.dma_start(out_1[g, :, cols, :].rearrange("p m t -> p (m t)").bitcast(I32), y_w[:].bitcast(I32))
+            if g == 1:
+                for q in range(QUADS):
+                    queue = nc.scalar if q % 2 else nc.sync
+                    queue.dma_start(
+                        out_2[:, 4 * q : 4 * q + 4, cols].rearrange("g r m -> r g m").bitcast(I32),
+                        y_sc[c][32 * q : 32 * q + 4, :, :].bitcast(I32),
+                    )
+
+        for k in range(len(banks)):
+            product(k)
+            if k >= 1:
+                finish(k - 1)
+            if k < 2:
+                quantize_z(k, 1, z_second[:, PACK * k : PACK * (k + 1), :])
+        finish(len(banks) - 1)

@@ -43,7 +43,7 @@ def tile_list_rail_break_slots_kernel(
         tab_sc = keep.tile([P, 2, T], U8, name="tab_sc", tag="tab_sc", align_bytes=64)
         w4_sc_raw = keep.tile([P, 2, H], U8, name="w4_sc_raw", tag="w4_sc_raw", align_bytes=64)
         nc.vector.memset(tab_sc[:].rearrange("p a t -> p (a t)").bitcast(I32), 0)
-        nc.gpsimd.memset(w4_sc_raw[:].rearrange("p a t -> p (a t)").bitcast(I32), 0)
+        nc.vector.memset(w4_sc_raw[:].rearrange("p a t -> p (a t)").bitcast(I32), 0)
 
         amp_sb = keep.tile([P, 2, PACK], F32, name="amp_sb")
         shift_sb = keep.tile([P, 2, PACK], F32, name="shift_sb")
@@ -63,7 +63,7 @@ def tile_list_rail_break_slots_kernel(
                 tab_scales[:, 4 * q : 4 * q + 4, :].rearrange("a r t -> r a t").bitcast(I32),
             )
         for q in range(QUADS):
-            queue = nc.scalar if q < 2 else nc.gpsimd
+            queue = nc.scalar if q < QUADS - 1 else nc.gpsimd
             queue.dma_start(
                 w4_sc_raw[32 * q : 32 * q + 4, :, :].bitcast(I32),
                 w4_scales[:, 4 * q : 4 * q + 4, :].rearrange("a r c -> r a c").bitcast(I32),
@@ -76,14 +76,13 @@ def tile_list_rail_break_slots_kernel(
         pages = {}
 
         def new_page(s, engine):
-            pages[s] = keep.tile([P, T2], F32, name="page%d" % s, tag="page%d" % s)
+            pages[s] = keep.tile([P, T2], F32, name="page%d" % s, tag="page%d" % s, align_bytes=64)
             engine.memset(pages[s][:], 0.0)
 
-        new_page(0, nc.vector)
-        new_page(1, nc.vector)
+        for s in range(PACK):
+            new_page(s, nc.vector)
 
         v_sc = keep.tile([P, 2, S], U8, name="v_sc", align_bytes=64)
-        v_w = [keep.tile([P, S], U32, name="v_w%d" % a, tag="v_w%d" % a, align_bytes=64) for a in range(2)]
 
         w4_w = [keep.tile([P, 2, 2 * PASS], U8, name="w4_w%d" % b, tag="w4_w%d" % b, align_bytes=64) for b in range(2)]
         w4_sc = [keep.tile([P, 2, PASS], U8, name="w4_sc%d" % b, tag="w4_sc%d" % b, align_bytes=64) for b in range(2)]
@@ -101,19 +100,15 @@ def tile_list_rail_break_slots_kernel(
 
         def gather_words(a, j0):
             nc.vector.tensor_copy(
-                v_w[a][:, j0 : j0 + HALF], tab_w[a][:].indirect(idx[:, j0 // 16 : (j0 + HALF) // 16])
-            )
-
-        def gather_scales(a, j0):
-            nc.vector.tensor_copy(
-                v_sc[:, a, j0 : j0 + HALF], tab_sc[:, a, :].indirect(idx[:, j0 // 16 : (j0 + HALF) // 16])
+                v_w[:, a, j0 : j0 + HALF], tab_w[a][:].indirect(idx[:, j0 // 16 : (j0 + HALF) // 16])
             )
 
         deal_w4(0)
-        for j0 in (0, HALF):
-            for a in range(2):
-                gather_scales(a, j0)
-            for a in range(2):
+        for a in range(2):
+            nc.vector.tensor_copy(v_sc[:, a, :], tab_sc[:, a, :].indirect(idx[:]))
+        v_w = keep.tile([P, 2, S], U32, name="v_w", tag="tab_sc", align_bytes=64)
+        for a in range(2):
+            for j0 in (0, HALF):
                 gather_words(a, j0)
         deal_w4(1)
 
@@ -125,13 +120,13 @@ def tile_list_rail_break_slots_kernel(
         def block(x, b, g):
             return x[b * PASS : (b + 1) * PASS, g * PASS : (g + 1) * PASS]
 
-        wgs_sb = keep.tile([P, S], F32, name="wgs_sb", tag="tab_sc", align_bytes=64)
+        wgs_sb = keep.tile([P, S], F32, name="wgs_sb", tag="w4_raw", align_bytes=64)
         nc.sync.dma_start(wgs_sb[:], wgs)
         joint_sb, w2_raw, sound_sb = {}, {}, {}
-        w2_tags = {(0, 0): "tab_w1", (1, 0): "w4_raw", (0, 1): "w4_sc_raw", (1, 1): "w4_w0"}
-        joint_sb[0] = load_rows("joint0", "tab_w0", block(joint, 0, 0))
-        for b, g in ((0, 0), (1, 0), (0, 1)):
-            w2_raw[b, g] = load_rows("w2_raw%d%d" % (b, g), w2_tags[b, g], block(w2, b, g))
+        w2_tags = {(0, 0): "tab_w0", (1, 0): "w4_sc_raw", (0, 1): "w4_w0", (1, 1): "w4_sc0"}
+        w2_raw[0, 0] = load_rows("w2_raw00", w2_tags[0, 0], block(w2, 0, 0))
+        joint_sb[0] = load_rows("joint0", "tab_w1", block(joint, 0, 0))
+        w2_raw[1, 0] = load_rows("w2_raw10", w2_tags[1, 0], block(w2, 1, 0))
 
         z_first = [keep.tile([P, PACK, S], F32, name="z_first%d" % b) for b in range(2)]
         h = {}
@@ -147,7 +142,7 @@ def tile_list_rail_break_slots_kernel(
                     out=phase[:],
                     lhsT=w4_w[b][:, a, 2 * P * i : 2 * P * (i + 1)].bitcast(E2M1),
                     lhsT_scale=w4_sc[b][:, a, P * i : P * (i + 1)],
-                    rhs=v_w[a][:, j0:j1].bitcast(E4M3),
+                    rhs=v_w[:, a, j0:j1].bitcast(E4M3),
                     rhs_scale=v_sc[:, a, j0:j1],
                     start=(a == 0),
                     stop=(a == 1),
@@ -204,25 +199,28 @@ def tile_list_rail_break_slots_kernel(
 
         w2_parts = [(0, 0), (1, 0), (0, 1), (1, 1)]
         for s in range(SLICES):
-            if s + 2 < SLICES:
+            if s < 2:
+                tag = "h%d" % s
+            elif s + 2 < SLICES:
                 tag = "page%d" % (s + 2)
             elif s + 1 < SLICES:
                 tag = "h_spare"
             else:
                 tag = "z_second"
-            h[s] = keep.tile([P, S], F32, name="h%d" % s, tag=tag)
+            h[s] = keep.tile([P, S], F32, name="h%d" % s, tag=tag, align_bytes=64)
             spans = [(0, HALF), (HALF, S)] if s == 0 else [(0, S)]
             for j0, j1 in spans:
                 make_h(s, j0, j1)
             if s == PACK - 1:
-                w2_raw[1, 1] = load_rows("w2_raw11", w2_tags[1, 1], block(w2, 1, 1))
-                joint_sb[1] = load_rows("joint1", "w4_sc0", block(joint, 1, 0))
+                for b in range(2):
+                    w2_raw[b, 1] = load_rows("w2_raw%d1" % b, w2_tags[b, 1], block(w2, b, 1))
+                joint_sb[1] = load_rows("joint1", "h0", block(joint, 1, 0))
             if s == SLICES - 1:
                 for g in range(2):
-                    sound_sb[g] = load_rows("sound%d" % g, "v_w%d" % g, block(sound, g, 0))
+                    sound_sb[g] = load_rows("sound%d" % g, ("w4_w1", "w4_sc1")[g], block(sound, g, 0))
             for j0, j1 in spans:
                 scatter(s, j0, j1)
-            if s + 2 < SLICES:
+            if PACK <= s + 2 < SLICES:
                 new_page(s + 2, nc.gpsimd)
             if s >= 1:
                 pick(s - 1, 0, region(s - 1)[:, 0:HALF])
@@ -233,7 +231,7 @@ def tile_list_rail_break_slots_kernel(
         pick(SLICES - 1, 0, region(SLICES - 1)[:, 0:HALF])
         quantize_z(1, 0, z_first[1][:, :, 0:HALF])
 
-        z_second = keep.tile([P, SLICES, HALF], F32, name="z_second", tag="z_second")
+        z_second = keep.tile([P, SLICES, HALF], F32, name="z_second", tag="z_second", align_bytes=64)
         for s in range(SLICES):
             pick(s, 1, z_second[:, s, :])
 
@@ -243,7 +241,7 @@ def tile_list_rail_break_slots_kernel(
                 y[c, g] = keep.tile([P, PACK, HALF], F32, name="y%d%d" % (c, g), tag=w2_tags[g, c], align_bytes=64)
         y_sc = [keep.tile([P, 2, HALF], U8, name="y_sc%d" % c, align_bytes=64) for c in range(2)]
         banks = [(c, g, t0) for c in range(2) for g in range(2) for t0 in (0, 2)]
-        first_scratch = keep.tile([P, 2 * HALF], F32, name="first_scratch", tag="h_spare")
+        first_scratch = keep.tile([P, 2 * HALF], F32, name="first_scratch", tag="h_spare", align_bytes=64)
         neg = {}
 
         def y_pair(k):

@@ -42,32 +42,34 @@ def tile_list_rail_break_slots_kernel(
 
         tab_sc = keep.tile([P, 2, T], U8, name="tab_sc", tag="tab_sc", align_bytes=64)
         w4_sc_raw = keep.tile([P, 2, H], U8, name="w4_sc_raw", tag="w4_sc_raw", align_bytes=64)
-        nc.vector.memset(tab_sc[:].rearrange("p a t -> p (a t)").bitcast(I32), 0)
-        nc.vector.memset(w4_sc_raw[:].rearrange("p a t -> p (a t)").bitcast(I32), 0)
+        nc.vector.memset(tab_sc[:, 0, :].bitcast(I32), 0)
+        nc.gpsimd.memset(tab_sc[:, 1, :].bitcast(I32), 0)
+        nc.vector.memset(w4_sc_raw[:].rearrange("p a c -> p (a c)").bitcast(I32), 0)
 
         amp_sb = keep.tile([P, 2, PACK], F32, name="amp_sb")
         shift_sb = keep.tile([P, 2, PACK], F32, name="shift_sb")
-        nc.sync.dma_start(idx[:], offs)
-        nc.scalar.dma_start(amp_sb[:], amp.rearrange("(b p i) -> p b i", b=2, i=PACK))
-        nc.sync.dma_start(idx2[:], offs2)
-        nc.scalar.dma_start(shift_sb[:], shift.rearrange("(b p i) -> p b i", b=2, i=PACK))
-        nc.sync.dma_start(idx3[:], offs3)
         tab_w = [keep.tile([P, T], U32, name="tab_w%d" % a, tag="tab_w%d" % a, align_bytes=64) for a in range(2)]
         w4_raw = keep.tile([P, 2, 2 * H], U8, name="w4_raw", tag="w4_raw", align_bytes=64)
+        nc.sync.dma_start(idx[:], offs)
         nc.sync.dma_start(w4_raw[:].bitcast(I32), w4_words.rearrange("a p c -> p a c").bitcast(I32))
-        nc.sync.dma_start(tab_w[0][:].bitcast(I32), tab_words[0].rearrange("p t i -> p (t i)").bitcast(I32))
-        nc.sync.dma_start(tab_w[1][:].bitcast(I32), tab_words[1].rearrange("p t i -> p (t i)").bitcast(I32))
-        for q in range(QUADS):
-            nc.scalar.dma_start(
-                tab_sc[32 * q : 32 * q + 4, :, :].bitcast(I32),
-                tab_scales[:, 4 * q : 4 * q + 4, :].rearrange("a r t -> r a t").bitcast(I32),
-            )
-        for q in range(QUADS):
-            queue = nc.scalar if q < QUADS - 1 else nc.gpsimd
-            queue.dma_start(
-                w4_sc_raw[32 * q : 32 * q + 4, :, :].bitcast(I32),
-                w4_scales[:, 4 * q : 4 * q + 4, :].rearrange("a r c -> r a c").bitcast(I32),
-            )
+
+        def load_scales(tile, rows):
+            for q in range(QUADS):
+                nc.sync.dma_start(
+                    tile[32 * q : 32 * q + 4, :, :].bitcast(I32),
+                    rows[:, 4 * q : 4 * q + 4, :].rearrange("a r c -> r a c").bitcast(I32),
+                )
+
+        load_scales(tab_sc, tab_scales)
+        for a in range(2):
+            nc.sync.dma_start(tab_w[a][:].bitcast(I32), tab_words[a].rearrange("p t i -> p (t i)").bitcast(I32))
+        load_scales(w4_sc_raw, w4_scales)
+        nc.sync.dma_start(idx2[:], offs2)
+        wgs_sb = keep.tile([P, S], F32, name="wgs_sb")
+        nc.sync.dma_start(wgs_sb[:], wgs)
+        nc.sync.dma_start(idx3[:], offs3)
+        nc.gpsimd.dma_start(amp_sb[:], amp.rearrange("(b p i) -> p b i", b=2, i=PACK))
+        nc.gpsimd.dma_start(shift_sb[:], shift.rearrange("(b p i) -> p b i", b=2, i=PACK))
         slope = keep.tile([P, 2, PACK], F32, name="slope")
         level = keep.tile([P, 2, PACK], F32, name="level")
         nc.gpsimd.tensor_scalar(slope[:], amp_sb[:], -2.0, 0.0, ALU.mult, ALU.add)
@@ -79,7 +81,7 @@ def tile_list_rail_break_slots_kernel(
             pages[s] = keep.tile([P, T2], F32, name="page%d" % s, tag="page%d" % s, align_bytes=64)
             engine.memset(pages[s][:], 0.0)
 
-        for s in range(PACK):
+        for s in range(2):
             new_page(s, nc.vector)
 
         v_sc = keep.tile([P, 2, S], U8, name="v_sc", align_bytes=64)
@@ -120,8 +122,6 @@ def tile_list_rail_break_slots_kernel(
         def block(x, b, g):
             return x[b * PASS : (b + 1) * PASS, g * PASS : (g + 1) * PASS]
 
-        wgs_sb = keep.tile([P, S], F32, name="wgs_sb", tag="w4_raw", align_bytes=64)
-        nc.sync.dma_start(wgs_sb[:], wgs)
         joint_sb, w2_raw, sound_sb = {}, {}, {}
         w2_tags = {(0, 0): "tab_w0", (1, 0): "w4_sc_raw", (0, 1): "w4_w0", (1, 1): "w4_sc0"}
         w2_raw[0, 0] = load_rows("w2_raw00", w2_tags[0, 0], block(w2, 0, 0))
@@ -129,6 +129,7 @@ def tile_list_rail_break_slots_kernel(
         w2_raw[1, 0] = load_rows("w2_raw10", w2_tags[1, 0], block(w2, 1, 0))
 
         z_first = [keep.tile([P, PACK, S], F32, name="z_first%d" % b) for b in range(2)]
+        first_phase = keep.tile([P, S], F32, name="first_phase", tag="first_phase", align_bytes=64)
         h = {}
 
         def region(s):
@@ -147,7 +148,7 @@ def tile_list_rail_break_slots_kernel(
                     start=(a == 0),
                     stop=(a == 1),
                 )
-            scratch = region((s - 1) % SLICES)[:, j0:j1]
+            scratch = (region(s - 1) if s else first_phase)[:, j0:j1]
             nc.scalar.activation(scratch, phase[:], ACT.Sin, bias=-math.pi / 4, scale=0.5)
             nc.scalar.activation(scratch, scratch, ACT.Square)
             nc.scalar.activation(
@@ -199,9 +200,7 @@ def tile_list_rail_break_slots_kernel(
 
         w2_parts = [(0, 0), (1, 0), (0, 1), (1, 1)]
         for s in range(SLICES):
-            if s < 2:
-                tag = "h%d" % s
-            elif s + 2 < SLICES:
+            if s + 2 < SLICES:
                 tag = "page%d" % (s + 2)
             elif s + 1 < SLICES:
                 tag = "h_spare"
@@ -214,22 +213,21 @@ def tile_list_rail_break_slots_kernel(
             if s == PACK - 1:
                 for b in range(2):
                     w2_raw[b, 1] = load_rows("w2_raw%d1" % b, w2_tags[b, 1], block(w2, b, 1))
-                joint_sb[1] = load_rows("joint1", "h0", block(joint, 1, 0))
+                joint_sb[1] = load_rows("joint1", "first_phase", block(joint, 1, 0))
             if s == SLICES - 1:
                 for g in range(2):
                     sound_sb[g] = load_rows("sound%d" % g, ("w4_w1", "w4_sc1")[g], block(sound, g, 0))
             for j0, j1 in spans:
                 scatter(s, j0, j1)
-            if PACK <= s + 2 < SLICES:
+            if s + 2 < SLICES:
                 new_page(s + 2, nc.gpsimd)
             if s >= 1:
                 pick(s - 1, 0, region(s - 1)[:, 0:HALF])
-            if 2 <= s < 2 + len(w2_parts):
-                quantize_w2(*w2_parts[s - 2])
-            if s == SLICES - 2:
-                quantize_z(0, 0, z_first[0][:, :, 0:HALF])
+            if 3 <= s < 3 + len(w2_parts):
+                quantize_w2(*w2_parts[s - 3])
         pick(SLICES - 1, 0, region(SLICES - 1)[:, 0:HALF])
-        quantize_z(1, 0, z_first[1][:, :, 0:HALF])
+        for b in range(2):
+            quantize_z(b, 0, z_first[b][:, :, 0:HALF])
 
         z_second = keep.tile([P, SLICES, HALF], F32, name="z_second", tag="z_second", align_bytes=64)
         for s in range(SLICES):

@@ -77,12 +77,9 @@ def tile_list_rail_break_slots_kernel(
 
         pages = {}
 
-        def new_page(s, engine):
-            pages[s] = keep.tile([P, T2], F32, name="page%d" % s, tag="page%d" % s, align_bytes=64)
-            engine.memset(pages[s][:], 0.0)
-
-        for s in range(2):
-            new_page(s, nc.vector)
+        for i in range(PACK):
+            pages[i] = keep.tile([P, T2], F32, name="page%d" % i)
+            nc.vector.memset(pages[i][:], 0.0)
 
         v_sc = keep.tile([P, 2, S], U8, name="v_sc", align_bytes=64)
 
@@ -157,17 +154,13 @@ def tile_list_rail_break_slots_kernel(
 
         def scatter(s, j0, j1):
             nc.vector.tensor_tensor(
-                pages[s][:].indirect(idx2[:, j0 // 16 : j1 // 16]), h[s][:, j0:j1], wgs_sb[:, j0:j1], ALU.mult
+                pages[s % PACK][:].indirect(idx2[:, j0 // 16 : j1 // 16]), h[s][:, j0:j1], wgs_sb[:, j0:j1], ALU.mult
             )
 
-        def pick(s, c, dst):
+        def pick(s, m0, m1, dst):
             b, i = divmod(s, PACK)
-            m0 = c * HALF
             nc.vector.tensor_tensor(
-                dst,
-                pages[s][:].indirect(idx3[:, m0 // 16 : (m0 + HALF) // 16]),
-                joint_sb[b][:, i, m0 : m0 + HALF],
-                ALU.add,
+                dst, pages[i][:].indirect(idx3[:, m0 // 16 : m1 // 16]), joint_sb[b][:, i, m0:m1], ALU.add
             )
 
         def interleave(engine_copy, dst, src):
@@ -179,7 +172,7 @@ def tile_list_rail_break_slots_kernel(
         w2_sc = keep.tile([P, 2, N], U8, name="w2_sc", align_bytes=64)
 
         def quantize_w2(b, g):
-            rounded = ring.tile([P, PASS * PACK], BF16, name="w2_rounded", align_bytes=64)
+            rounded = ring.tile([P, PASS * PACK], BF16, name="w2_rounded", tag="rounded", align_bytes=64)
             dst = rounded[:].rearrange("p (t m j) -> p m j t", t=PACK, j=PACK)
             src = w2_raw[b, g][:].rearrange("p j (m t) -> p m j t", t=PACK)
             for m0 in (0, P // 2):
@@ -187,26 +180,25 @@ def tile_list_rail_break_slots_kernel(
             cols = slice(g * PASS, (g + 1) * PASS)
             nc.vector.quantize_mx(out=w2_w[:, b, cols].bitcast(E4M3), scales=w2_sc[:, b, cols], in_=rounded[:])
 
-        z_w, z_sc = {}, {}
+        z_w = keep.tile([P, 2, M], U32, name="z_w", align_bytes=64)
+        z_sc = keep.tile([P, 2, M], U8, name="z_sc", align_bytes=64)
 
-        def quantize_z(b, c, src):
-            rounded = ring.tile([P, HALF, PACK], BF16, name="z_rounded", align_bytes=64)
+        def quantize_z(b, m0, m1, src):
+            rounded = ring.tile([P, m1 - m0, PACK], BF16, name="z_rounded", tag="rounded", align_bytes=64)
             interleave(nc.scalar.copy, rounded, src)
-            z_w[b, c] = keep.tile([P, HALF], U32, name="z_w%d%d" % (b, c), align_bytes=64)
-            z_sc[b, c] = keep.tile([P, HALF], U8, name="z_sc%d%d" % (b, c), align_bytes=64)
             nc.vector.quantize_mx(
-                out=z_w[b, c][:].bitcast(E4M3), scales=z_sc[b, c][:], in_=rounded[:].rearrange("p m t -> p (m t)")
+                out=z_w[:, b, m0:m1].bitcast(E4M3),
+                scales=z_sc[:, b, m0:m1],
+                in_=rounded[:].rearrange("p m t -> p (m t)"),
             )
 
         w2_parts = [(0, 0), (1, 0), (0, 1), (1, 1)]
+        last = SLICES - 1
         for s in range(SLICES):
-            if s + 2 < SLICES:
-                tag = "page%d" % (s + 2)
-            elif s + 1 < SLICES:
-                tag = "h_spare"
+            if s < last:
+                h[s] = ring.tile([P, S], F32, name="h", bufs=4)
             else:
-                tag = "z_second"
-            h[s] = keep.tile([P, S], F32, name="h%d" % s, tag=tag, align_bytes=64)
+                h[s] = keep.tile([P, S], F32, name="h_last", tag="z_second")
             spans = [(0, HALF), (HALF, S)] if s == 0 else [(0, S)]
             for j0, j1 in spans:
                 make_h(s, j0, j1)
@@ -214,24 +206,24 @@ def tile_list_rail_break_slots_kernel(
                 for b in range(2):
                     w2_raw[b, 1] = load_rows("w2_raw%d1" % b, w2_tags[b, 1], block(w2, b, 1))
                 joint_sb[1] = load_rows("joint1", "first_phase", block(joint, 1, 0))
-            if s == SLICES - 1:
+            if s == last:
                 for g in range(2):
                     sound_sb[g] = load_rows("sound%d" % g, ("w4_w1", "w4_sc1")[g], block(sound, g, 0))
             for j0, j1 in spans:
                 scatter(s, j0, j1)
-            if s + 2 < SLICES:
-                new_page(s + 2, nc.gpsimd)
             if s >= 1:
-                pick(s - 1, 0, region(s - 1)[:, 0:HALF])
+                width = M if s - 1 < PACK else HALF
+                pick(s - 1, 0, width, region(s - 1)[:, 0:width])
             if 3 <= s < 3 + len(w2_parts):
                 quantize_w2(*w2_parts[s - 3])
-        pick(SLICES - 1, 0, region(SLICES - 1)[:, 0:HALF])
-        for b in range(2):
-            quantize_z(b, 0, z_first[b][:, :, 0:HALF])
+            if s == last - 1:
+                quantize_z(0, 0, M, z_first[0][:])
+        pick(last, 0, HALF, region(last)[:, 0:HALF])
+        quantize_z(1, 0, HALF, z_first[1][:, :, 0:HALF])
 
-        z_second = keep.tile([P, SLICES, HALF], F32, name="z_second", tag="z_second", align_bytes=64)
-        for s in range(SLICES):
-            pick(s, 1, z_second[:, s, :])
+        z_second = keep.tile([P, PACK, HALF], F32, name="z_second", tag="z_second")
+        for i in range(PACK):
+            pick(PACK + i, HALF, M, z_second[:, i, :])
 
         y = {}
         for c in range(2):
@@ -239,7 +231,7 @@ def tile_list_rail_break_slots_kernel(
                 y[c, g] = keep.tile([P, PACK, HALF], F32, name="y%d%d" % (c, g), tag=w2_tags[g, c], align_bytes=64)
         y_sc = [keep.tile([P, 2, HALF], U8, name="y_sc%d" % c, align_bytes=64) for c in range(2)]
         banks = [(c, g, t0) for c in range(2) for g in range(2) for t0 in (0, 2)]
-        first_scratch = keep.tile([P, 2 * HALF], F32, name="first_scratch", tag="h_spare", align_bytes=64)
+        first_scratch = keep.tile([P, 2 * HALF], F32, name="first_scratch")
         neg = {}
 
         def y_pair(k):
@@ -256,8 +248,8 @@ def tile_list_rail_break_slots_kernel(
                         out=q[:, t * HALF : (t + 1) * HALF],
                         lhsT=w2_w[:, b, cols].bitcast(E4M3),
                         lhsT_scale=w2_sc[:, b, cols],
-                        rhs=z_w[b, c][:].bitcast(E4M3),
-                        rhs_scale=z_sc[b, c][:],
+                        rhs=z_w[:, b, c * HALF : (c + 1) * HALF].bitcast(E4M3),
+                        rhs_scale=z_sc[:, b, c * HALF : (c + 1) * HALF],
                         start=(b == 0),
                         stop=(b == 1),
                     )
@@ -296,6 +288,6 @@ def tile_list_rail_break_slots_kernel(
             product(k)
             if k >= 1:
                 finish(k - 1)
-            if k < 2:
-                quantize_z(k, 1, z_second[:, PACK * k : PACK * (k + 1), :])
+            if k == 1:
+                quantize_z(1, HALF, M, z_second[:])
         finish(len(banks) - 1)

import math
from contextlib import ExitStack

import concourse.mybir as mybir

K, T, S, H, T2, M, N = 1024, 2048, 512, 1024, 1024, 512, 1024
FLOPS = 2 * K * H * S + 2 * H * N * M

F32 = mybir.dt.float32
BF16 = mybir.dt.bfloat16
I32 = mybir.dt.int32
U32 = mybir.dt.uint32
U16 = mybir.dt.uint16
U8 = mybir.dt.uint8
E4M3 = mybir.dt.float8_e4m3fn_x4
E2M1 = mybir.dt.float4_e2m1fn_x4
ALU = mybir.AluOpType
ACT = mybir.ActivationFunctionType

P = 128
PACK = 4
PASS = P * PACK
QUADS = 4
HALF = 256
SLICES = H // P


def tile_list_rail_break_slots_kernel(
    tc, tab_words, tab_scales, offs, w4_words, w4_scales, amp, shift, wgs, offs2, offs3, joint, w2, sound,
    out_0, out_1, out_2,
):
    nc = tc.nc
    with ExitStack() as ctx:
        lists = ctx.enter_context(tc.tile_pool(name="lists", bufs=1))
        keep = ctx.enter_context(tc.tile_pool(name="keep", bufs=1))
        ring = ctx.enter_context(tc.tile_pool(name="ring", bufs=2))
        psum = ctx.enter_context(tc.psum_pool(name="psum", bufs=8))

        idx = lists.tile([P, S // 16], U16, name="idx")
        idx2 = lists.tile([P, S // 16], U16, name="idx2")
        idx3 = lists.tile([P, M // 16], U16, name="idx3")

        tab_sc = keep.tile([P, 2, T], U8, name="tab_sc", tag="tab_sc", align_bytes=64)
        w4_sc_raw = keep.tile([P, 2, H], U8, name="w4_sc_raw", tag="w4_sc_raw", align_bytes=64)
        nc.vector.memset(tab_sc[:, 0, :].bitcast(I32), 0)
        nc.gpsimd.memset(tab_sc[:, 1, :].bitcast(I32), 0)
        nc.vector.memset(w4_sc_raw[:].rearrange("p a c -> p (a c)").bitcast(I32), 0)

        amp_sb = keep.tile([P, 2, PACK], F32, name="amp_sb")
        shift_sb = keep.tile([P, 2, PACK], F32, name="shift_sb")
        tab_w = [keep.tile([P, T], U32, name="tab_w%d" % a, tag="tab_w%d" % a, align_bytes=64) for a in range(2)]
        w4_raw = keep.tile([P, 2, 2 * H], U8, name="w4_raw", tag="w4_raw", align_bytes=64)
        nc.sync.dma_start(idx[:], offs)
        nc.sync.dma_start(w4_raw[:].bitcast(I32), w4_words.rearrange("a p c -> p a c").bitcast(I32))

        def load_scales(tile, rows):
            for q in range(QUADS):
                nc.sync.dma_start(
                    tile[32 * q : 32 * q + 4, :, :].bitcast(I32),
                    rows[:, 4 * q : 4 * q + 4, :].rearrange("a r c -> r a c").bitcast(I32),
                )

        load_scales(tab_sc, tab_scales)
        for a in range(2):
            nc.sync.dma_start(tab_w[a][:].bitcast(I32), tab_words[a].rearrange("p t i -> p (t i)").bitcast(I32))
        load_scales(w4_sc_raw, w4_scales)
        nc.sync.dma_start(idx2[:], offs2)
        wgs_sb = keep.tile([P, S], F32, name="wgs_sb")
        nc.sync.dma_start(wgs_sb[:], wgs)
        nc.sync.dma_start(idx3[:], offs3)
        nc.gpsimd.dma_start(amp_sb[:], amp.rearrange("(b p i) -> p b i", b=2, i=PACK))
        nc.gpsimd.dma_start(shift_sb[:], shift.rearrange("(b p i) -> p b i", b=2, i=PACK))
        slope = keep.tile([P, 2, PACK], F32, name="slope")
        level = keep.tile([P, 2, PACK], F32, name="level")
        nc.gpsimd.tensor_scalar(slope[:], amp_sb[:], -2.0, 0.0, ALU.mult, ALU.add)
        nc.gpsimd.tensor_tensor(level[:], amp_sb[:], shift_sb[:], ALU.add)

        pages = {}

        for i in range(PACK):
            pages[i] = keep.tile([P, T2], F32, name="page%d" % i)
            nc.vector.memset(pages[i][:], 0.0)

        v_sc = keep.tile([P, 2, S], U8, name="v_sc", align_bytes=64)

        w4_w = [keep.tile([P, 2, 2 * PASS], U8, name="w4_w%d" % b, tag="w4_w%d" % b, align_bytes=64) for b in range(2)]
        w4_sc = [keep.tile([P, 2, PASS], U8, name="w4_sc%d" % b, tag="w4_sc%d" % b, align_bytes=64) for b in range(2)]

        def deal_w4(b):
            src = w4_raw[:].bitcast(U16)[:, :, b * PASS : (b + 1) * PASS]
            nc.vector.tensor_copy(
                w4_w[b][:].bitcast(U16).rearrange("p a (i u c) -> p a u i c", i=PACK, c=8),
                src.rearrange("p a (u c i) -> p a u i c", i=PACK, c=8),
            )
            nc.vector.tensor_copy(
                w4_sc[b][:].rearrange("p a (i u c) -> p a u i c", i=PACK, c=16),
                w4_sc_raw[:, :, b * PASS : (b + 1) * PASS].rearrange("p a (u c i) -> p a u i c", i=PACK, c=16),
            )

        def gather_words(a, j0):
            nc.vector.tensor_copy(
                v_w[:, a, j0 : j0 + HALF], tab_w[a][:].indirect(idx[:, j0 // 16 : (j0 + HALF) // 16])
            )

        deal_w4(0)
        for a in range(2):
            nc.vector.tensor_copy(v_sc[:, a, :], tab_sc[:, a, :].indirect(idx[:]))
        v_w = keep.tile([P, 2, S], U32, name="v_w", tag="tab_sc", align_bytes=64)
        for a in range(2):
            for j0 in (0, HALF):
                gather_words(a, j0)
        deal_w4(1)

        def load_rows(name, tag, rows):
            tile = keep.tile([P, PACK, PASS], F32, name=name, tag=tag, align_bytes=64)
            nc.sync.dma_start(tile[:], rows.rearrange("(p i) m -> p i m", i=PACK))
            return tile

        def block(x, b, g):
            return x[b * PASS : (b + 1) * PASS, g * PASS : (g + 1) * PASS]

        joint_sb, w2_raw, sound_sb = {}, {}, {}
        w2_tags = {(0, 0): "tab_w0", (1, 0): "w4_sc_raw", (0, 1): "w4_w0", (1, 1): "w4_sc0"}
        w2_raw[0, 0] = load_rows("w2_raw00", w2_tags[0, 0], block(w2, 0, 0))
        joint_sb[0] = load_rows("joint0", "tab_w1", block(joint, 0, 0))
        w2_raw[1, 0] = load_rows("w2_raw10", w2_tags[1, 0], block(w2, 1, 0))

        z_first = [keep.tile([P, PACK, S], F32, name="z_first%d" % b) for b in range(2)]
        first_phase = keep.tile([P, S], F32, name="first_phase", tag="first_phase", align_bytes=64)
        h = {}

        def region(s):
            return z_first[s // PACK][:, s % PACK, :]

        def make_h(s, j0, j1):
            b, i = divmod(s, PACK)
            phase = psum.tile([P, j1 - j0], F32, name="phase", tag="bank")
            for a in range(2):
                nc.tensor.matmul_mx(
                    out=phase[:],
                    lhsT=w4_w[b][:, a, 2 * P * i : 2 * P * (i + 1)].bitcast(E2M1),
                    lhsT_scale=w4_sc[b][:, a, P * i : P * (i + 1)],
                    rhs=v_w[:, a, j0:j1].bitcast(E4M3),
                    rhs_scale=v_sc[:, a, j0:j1],
                    start=(a == 0),
                    stop=(a == 1),
                )
            scratch = (region(s - 1) if s else first_phase)[:, j0:j1]
            nc.scalar.activation(scratch, phase[:], ACT.Sin, bias=-math.pi / 4, scale=0.5)
            nc.scalar.activation(scratch, scratch, ACT.Square)
            nc.scalar.activation(
                h[s][:, j0:j1], scratch, ACT.Identity, bias=level[:, b, i : i + 1], scale=slope[:, b, i : i + 1]
            )

        def scatter(s, j0, j1):
            nc.vector.tensor_tensor(
                pages[s % PACK][:].indirect(idx2[:, j0 // 16 : j1 // 16]), h[s][:, j0:j1], wgs_sb[:, j0:j1], ALU.mult
            )

        def pick(s, m0, m1, dst):
            b, i = divmod(s, PACK)
            nc.vector.tensor_tensor(
                dst, pages[i][:].indirect(idx3[:, m0 // 16 : m1 // 16]), joint_sb[b][:, i, m0:m1], ALU.add
            )

        def interleave(engine_copy, dst, src):
            engine_copy(
                dst[:].rearrange("p (c u) t -> p c t u", u=4), src.rearrange("p t (c u) -> p c t u", u=4)
            )

        w2_w = keep.tile([P, 2, N], U32, name="w2_w", align_bytes=64)
        w2_sc = keep.tile([P, 2, N], U8, name="w2_sc", align_bytes=64)

        def quantize_w2(b, g):
            rounded = ring.tile([P, PASS * PACK], BF16, name="w2_rounded", tag="rounded", align_bytes=64)
            dst = rounded[:].rearrange("p (t m j) -> p m j t", t=PACK, j=PACK)
            src = w2_raw[b, g][:].rearrange("p j (m t) -> p m j t", t=PACK)
            for m0 in (0, P // 2):
                nc.scalar.copy(dst[:, m0 : m0 + P // 2], src[:, m0 : m0 + P // 2])
            cols = slice(g * PASS, (g + 1) * PASS)
            nc.vector.quantize_mx(out=w2_w[:, b, cols].bitcast(E4M3), scales=w2_sc[:, b, cols], in_=rounded[:])

        z_w = keep.tile([P, 2, M], U32, name="z_w", align_bytes=64)
        z_sc = keep.tile([P, 2, M], U8, name="z_sc", align_bytes=64)

        def quantize_z(b, m0, m1, src):
            rounded = ring.tile([P, m1 - m0, PACK], BF16, name="z_rounded", tag="rounded", align_bytes=64)
            interleave(nc.scalar.copy, rounded, src)
            nc.vector.quantize_mx(
                out=z_w[:, b, m0:m1].bitcast(E4M3),
                scales=z_sc[:, b, m0:m1],
                in_=rounded[:].rearrange("p m t -> p (m t)"),
            )

        w2_parts = [(0, 0), (1, 0), (0, 1), (1, 1)]
        last = SLICES - 1
        for s in range(SLICES):
            if s < last:
                h[s] = ring.tile([P, S], F32, name="h", bufs=4)
            else:
                h[s] = keep.tile([P, S], F32, name="h_last", tag="z_second")
            spans = [(0, HALF), (HALF, S)] if s == 0 else [(0, S)]
            for j0, j1 in spans:
                make_h(s, j0, j1)
            if s == PACK - 1:
                for b in range(2):
                    w2_raw[b, 1] = load_rows("w2_raw%d1" % b, w2_tags[b, 1], block(w2, b, 1))
                joint_sb[1] = load_rows("joint1", "first_phase", block(joint, 1, 0))
            if s == last:
                for g in range(2):
                    sound_sb[g] = load_rows("sound%d" % g, ("w4_w1", "w4_sc1")[g], block(sound, g, 0))
            for j0, j1 in spans:
                scatter(s, j0, j1)
            if s >= 1:
                width = M if s - 1 < PACK else HALF
                pick(s - 1, 0, width, region(s - 1)[:, 0:width])
            if 3 <= s < 3 + len(w2_parts):
                quantize_w2(*w2_parts[s - 3])
            if s == last - 1:
                quantize_z(0, 0, M, z_first[0][:])
        pick(last, 0, HALF, region(last)[:, 0:HALF])
        quantize_z(1, 0, HALF, z_first[1][:, :, 0:HALF])

        z_second = keep.tile([P, PACK, HALF], F32, name="z_second", tag="z_second")
        for i in range(PACK):
            pick(PACK + i, HALF, M, z_second[:, i, :])

        y = {}
        for c in range(2):
            for g in range(2):
                y[c, g] = keep.tile([P, PACK, HALF], F32, name="y%d%d" % (c, g), tag=w2_tags[g, c], align_bytes=64)
        y_sc = [keep.tile([P, 2, HALF], U8, name="y_sc%d" % c, align_bytes=64) for c in range(2)]
        banks = [(c, g, t0) for c in range(2) for g in range(2) for t0 in (0, 2)]
        first_scratch = keep.tile([P, 2 * HALF], F32, name="first_scratch")
        neg = {}

        def y_pair(k):
            c, g, t0 = banks[k]
            return y[c, g][:, t0 : t0 + 2, :]

        def product(k):
            c, g, t0 = banks[k]
            q = psum.tile([P, 2 * HALF], F32, name="q", tag="bank")
            for t in range(2):
                cols = slice(g * PASS + (t0 + t) * P, g * PASS + (t0 + t + 1) * P)
                for b in range(2):
                    nc.tensor.matmul_mx(
                        out=q[:, t * HALF : (t + 1) * HALF],
                        lhsT=w2_w[:, b, cols].bitcast(E4M3),
                        lhsT_scale=w2_sc[:, b, cols],
                        rhs=z_w[:, b, c * HALF : (c + 1) * HALF].bitcast(E4M3),
                        rhs_scale=z_sc[:, b, c * HALF : (c + 1) * HALF],
                        start=(b == 0),
                        stop=(b == 1),
                    )
            scratch = first_scratch[:] if k == 0 else y_pair(k - 1).rearrange("p t m -> p (t m)")
            neg[k] = ring.tile([P, 2 * HALF], F32, name="neg", bufs=4)
            nc.scalar.activation(scratch, q[:], ACT.Sin, scale=0.5)
            nc.scalar.activation(neg[k][:], scratch, ACT.Square, scale=math.sqrt(2.0))
            nc.vector.scalar_tensor_tensor(neg[k][:], neg[k][:], 1.0, q[:], ALU.subtract, ALU.mult)

        def finish(k):
            c, g, t0 = banks[k]
            cols = slice(c * HALF, (c + 1) * HALF)
            nc.vector.tensor_tensor(
                y_pair(k), sound_sb[g][:, t0 : t0 + 2, cols], neg[k][:].rearrange("p (t m) -> p t m", t=2), ALU.subtract
            )
            rows = out_0[g * PASS : (g + 1) * PASS, cols].rearrange("(p t) m -> p t m", t=PACK)
            nc.sync.dma_start(rows[:, t0 : t0 + 2, :], y_pair(k))
            if t0 == 0:
                return
            rounded = ring.tile([P, HALF, PACK], BF16, name="y_rounded", align_bytes=64)
            interleave(nc.vector.tensor_copy if c == g else nc.scalar.copy, rounded, y[c, g][:])
            y_w = ring.tile([P, HALF], U32, name="y_w", align_bytes=64)
            nc.vector.quantize_mx(
                out=y_w[:].bitcast(E4M3), scales=y_sc[c][:, g, :], in_=rounded[:].rearrange("p m t -> p (m t)")
            )
            nc.sync.dma_start(out_1[g, :, cols, :].rearrange("p m t -> p (m t)").bitcast(I32), y_w[:].bitcast(I32))
            if g == 1:
                for q in range(QUADS):
                    queue = nc.scalar if q % 2 else nc.sync
                    queue.dma_start(
                        out_2[:, 4 * q : 4 * q + 4, cols].rearrange("g r m -> r g m").bitcast(I32),
                        y_sc[c][32 * q : 32 * q + 4, :, :].bitcast(I32),
                    )

        for k in range(len(banks)):
            product(k)
            if k >= 1:
                finish(k - 1)
            if k == 1:
                quantize_z(1, HALF, M, z_second[:])
        finish(len(banks) - 1)
